import numpy as np
import ml_dtypes


def mxq(x, axis, fmt="e4m3"):
    dtype, down = {"e4m3": (ml_dtypes.float8_e4m3fn, 7), "e5m2": (ml_dtypes.float8_e5m2, 14)}[fmt]
    v = np.moveaxis(np.asarray(x, np.float32).astype(ml_dtypes.bfloat16).astype(np.float64), axis, -1)
    blocks = v.reshape(v.shape[:-1] + (-1, 32))
    amax = np.abs(blocks).max(-1, keepdims=True)
    byte = np.maximum(np.where(amax > 0, np.frexp(amax)[1] - 1 + 127, 0) - down, 1)
    scale = np.exp2(byte - 127.0)
    codes = (blocks / scale).astype(np.float32).astype(dtype).astype(np.float64)
    return np.moveaxis((codes * scale).reshape(v.shape), -1, axis)


WIDE = False


def mx_kscale(k):
    if not WIDE:
        return np.ones(k)
    levels = np.array([10, -10, 5, -5, 0])
    if k % 512:
        return np.exp2(np.random.permutation(np.resize(levels, k // 32))).repeat(32)
    a = np.empty((k // 512, 16))
    for p in range(k // 512):
        a[p, :8] = np.random.permutation(np.resize(levels, 8))
        for g in range(8):
            far = levels[np.abs(levels - a[p, g]) >= 10]
            a[p, g + 8] = far[np.random.randint(len(far))]
    return np.exp2(a.ravel()).repeat(32)


def f64(x):
    return np.asarray(x).astype(np.float64)


def striped(idx):
    return np.tile(idx.reshape(-1, 16).T, (8, 1)).astype(np.uint16)


def unstriped(offs):
    return offs[:16].T.reshape(-1).astype(np.int64)


def silu(v):
    return v / (1.0 + np.exp(-np.maximum(v, -700.0)))


K, T, S, D, V, H, N = 512, 1024, 512, 2, 256, 512, 256
P = 2 ** 7


def setup_inputs():
    n = np.random.standard_normal
    s = mx_kscale(K)[:, None]
    u = mx_kscale(H)
    return {
        "xT": (n((K, T)) * s).astype(np.float32),
        "w1": (n((K, H)) / np.sqrt(K) / s * u).astype(np.float32),
        "w2": (n((H, N)) / np.sqrt(H) / u[:, None]).astype(np.float32),
        "gate": (np.tile(np.random.uniform(0.2, 1.0, (D, 1, V)) / np.sqrt(D), (1, P, 1))).astype(np.float32),
        "offs": striped(np.random.permutation(T)[:S]),
        "cen": striped(np.random.permutation(S)[:V]),
        "pos1": striped(np.random.permutation(S)[:V]),
        "pos2": striped(np.random.permutation(S)[:V]),
    }


def reference(xT, w1, w2, gate, offs, cen, pos1, pos2):
    xq = mxq(f64(xT)[:, unstriped(offs)], 0, "e4m3")
    h = silu(mxq(f64(w1), 0, "e4m3").T @ xq)
    z = h[:, unstriped(cen)] - (h[:, unstriped(pos1)] * f64(gate)[0, :1] + h[:, unstriped(pos2)] * f64(gate)[1, :1])
    return mxq(f64(w2), 0, "e4m3").T @ mxq(z, 0, "e4m3")

@@ -1,0 +1,175 @@
+from contextlib import ExitStack
+
+import concourse.mybir as mybir
+from concourse.masks import make_identity
+
+K, T, S, V, H, N = 512, 1024, 512, 256, 512, 256
+FLOPS = 2 * K * H * S + 2 * H * N * V
+
+F32 = mybir.dt.float32
+BF16 = mybir.dt.bfloat16
+U32 = mybir.dt.uint32
+U16 = mybir.dt.uint16
+U8 = mybir.dt.uint8
+FP8X4 = mybir.dt.float8_e4m3fn_x4
+ACT = mybir.ActivationFunctionType
+ALU = mybir.AluOpType
+
+P = 128
+PACK = 4
+
+
+def weave(copy, woven, rows):
+    copy(
+        out=woven.rearrange("p (c i) j -> p c j i", i=4),
+        in_=rows.rearrange("p j (c i) -> p c j i", i=4),
+    )
+
+
+def quantize(nc, pool, woven, name):
+    width = woven.shape[1]
+    codes = pool.tile([P, width], U32, align_bytes=64, name=name + "_codes")
+    scales = pool.tile([P, width], U8, align_bytes=64, name=name + "_scales")
+    nc.vector.quantize_mx(out=codes[:].bitcast(FP8X4), scales=scales[:], in_=woven.rearrange("p w j -> p (w j)"))
+    return codes, scales
+
+
+def mx(nc, out, lhs, cols, rhs):
+    nc.tensor.matmul_mx(
+        out=out, lhsT=lhs[0][:, cols].bitcast(FP8X4), lhsT_scale=lhs[1][:, cols],
+        rhs=rhs[0][:].bitcast(FP8X4), rhs_scale=rhs[1][:], start=True, stop=True,
+    )
+
+
+def tile_picked_lapl_silu_e_kernel(tc, xT, w1, w2, gate, offs, cen, pos1, pos2, out):
+    nc = tc.nc
+    with ExitStack() as ctx:
+        lists = ctx.enter_context(tc.tile_pool(name="lists", bufs=1))
+        keep = ctx.enter_context(tc.tile_pool(name="keep", bufs=1))
+        psum = ctx.enter_context(tc.psum_pool(name="psum", bufs=1))
+
+        offs_t = lists.tile([P, S // 16], U16, name="offs_t")
+        cen_t = lists.tile([P, V // 16], U16, name="cen_t")
+        pos1_t = lists.tile([P, V // 16], U16, name="pos1_t")
+        pos2_t = lists.tile([P, V // 16], U16, name="pos2_t")
+
+        x_rows = xT.rearrange("(p j) t -> p j t", j=PACK)
+        w1_rows = w1.rearrange("(p j) i -> p j i", j=PACK)
+        xp = [keep.tile([P, T], F32, name="xp%d" % j) for j in range(PACK)]
+        w1r = [keep.tile([P, PACK, 256], F32, name="w1r%d" % c) for c in range(2)]
+        gate_t = keep.tile([P, 2, V], F32, name="gate_t")
+        w2r = keep.tile([P, PACK, N], F32, name="w2r")
+
+        nc.sync.dma_start(xp[0][:], x_rows[:, 0, :])
+        nc.sync.dma_start(offs_t[:], offs)
+        for j in range(1, PACK):
+            nc.sync.dma_start(xp[j][:], x_rows[:, j, :])
+        nc.sync.dma_start(w1r[0][:], w1_rows[:, :, 0:256])
+        nc.sync.dma_start(gate_t[:], gate.rearrange("d p v -> p d v"))
+        nc.sync.dma_start(w1r[1][:], w1_rows[:, :, 256:512])
+        nc.sync.dma_start(cen_t[:], cen)
+        nc.sync.dma_start(pos1_t[:], pos1)
+        nc.sync.dma_start(pos2_t[:], pos2)
+        nc.sync.dma_start(w2r[:], w2.rearrange("(p j) m -> p j m", j=PACK))
+
+        ident = keep.tile([P, P], F32, name="ident")
+        make_identity(nc, ident[:])
+        zero_in = keep.tile([P, 1], F32, name="zero_in")
+        zero = keep.tile([P, 1], F32, name="zero")
+        nc.vector.memset(zero_in[:], 0.0)
+        nc.scalar.activation(out=zero[:], in_=zero_in[:], func=ACT.Silu)
+
+        xg = [keep.tile([P, PACK, 256], F32, name="xg%d" % a) for a in range(2)]
+        for j in range(PACK):
+            for a in range(2):
+                nc.vector.tensor_copy(out=xg[a][:, j, :], in_=xp[j][:].indirect(offs_t[:, 16 * a : 16 * a + 16]))
+
+        w1w = [keep.tile([P, P, PACK], BF16, align_bytes=64, name="w1w%d" % t) for t in range(4)]
+        xw = [keep.tile([P, 256, PACK], BF16, align_bytes=64, name="xw%d" % a) for a in range(2)]
+
+        def w1_cols(t):
+            return w1r[t // 2][:, :, (t % 2) * P : (t % 2 + 1) * P]
+
+        weave(nc.scalar.copy, w1w[0][:], w1_cols(0))
+        weave(nc.scalar.copy, xw[0][:], xg[0][:])
+        w1q = [quantize(nc, keep, w1w[0][:], "w1q0")]
+        weave(nc.vector.tensor_copy, xw[1][:], xg[1][:])
+        xq = [None, None]
+        xq[1] = quantize(nc, keep, xw[1][:], "xq1")
+        xq[0] = quantize(nc, keep, xw[0][:], "xq0")
+
+        h = [keep.tile([P, S], F32, name="h%d" % t) for t in range(4)]
+        allc = slice(0, P)
+        for a in (1, 0):
+            acc = psum.tile([P, 256], F32, tag="acc", bufs=3, name="acc0_%d" % a)
+            mx(nc, acc[:], w1q[0], allc, xq[a])
+            nc.scalar.activation(out=h[0][:, 256 * a : 256 * a + 256], in_=acc[:], func=ACT.Silu, bias=zero[:])
+
+        ngate = keep.tile([P, 2, V], F32, name="ngate")
+        nc.vector.tensor_scalar(out=ngate[:], in0=gate_t[:], scalar1=-1.0, scalar2=None, op0=ALU.mult)
+        weave(nc.vector.tensor_copy, w1w[1][:], w1_cols(1))
+        w1q.append(quantize(nc, keep, w1w[1][:], "w1q1"))
+
+        def hidden(t):
+            acc = psum.tile([P, 2, 256], F32, tag="acc", bufs=3, name="acc%d" % t)
+            for a in range(2):
+                mx(nc, acc[:, a, :], w1q[t], allc, xq[a])
+            nc.scalar.activation(out=h[t][:], in_=acc[:].rearrange("p a s -> p (a s)"), func=ACT.Silu, bias=zero[:])
+
+        zt = [keep.tile([P, 2, P, 2], BF16, name="zt%d" % a) for a in range(2)]
+
+        def gather3(t, lo, n):
+            cols = slice(lo // 16, (lo + n) // 16)
+            c = keep.tile([P, n], F32, name="c%d_%d" % (t, lo))
+            d0 = keep.tile([P, n], F32, name="d0%d_%d" % (t, lo))
+            d1 = keep.tile([P, n], F32, name="d1%d_%d" % (t, lo))
+            nc.vector.tensor_copy(out=c[:], in_=h[t][:].indirect(cen_t[:, cols]))
+            nc.vector.tensor_tensor(out=d0[:], in0=h[t][:].indirect(pos1_t[:, cols]), in1=ngate[:, 0, lo : lo + n], op=ALU.mult)
+            nc.vector.tensor_tensor(out=d1[:], in0=h[t][:].indirect(pos2_t[:, cols]), in1=ngate[:, 1, lo : lo + n], op=ALU.mult)
+            return c, d0, d1
+
+        def add_turned(t, a, terms, lo):
+            turned = psum.tile([P, P], F32, tag="turned", bufs=2, name="turned%d_%d" % (t, a))
+            for n, term in enumerate(terms):
+                nc.tensor.matmul(turned[:], term[:, lo : lo + P], ident[:], start=(n == 0), stop=(n == 2), is_transpose=True)
+            nc.scalar.copy(
+                out=zt[a][:, :, 32 * t : 32 * t + 32, :],
+                in_=turned[:].rearrange("v (q u e) -> v u q e", u=2, e=2),
+            )
+
+        hidden(1)
+        w2w = keep.tile([P, N, PACK], BF16, align_bytes=64, name="w2w")
+        for t in range(3):
+            terms = gather3(t, 0, V)
+            if t < 2:
+                weave(nc.scalar.copy, w1w[t + 2][:], w1_cols(t + 2))
+                w1q.append(quantize(nc, keep, w1w[t + 2][:], "w1q%d" % (t + 2)))
+                hidden(t + 2)
+            else:
+                weave(nc.scalar.copy, w2w[:], w2r[:])
+            for a in range(2):
+                add_turned(t, a, terms, a * P)
+
+        out_v = out.rearrange("(c p) v -> p c v", p=P)
+        last = [gather3(3, 0, P)]
+        w2q = quantize(nc, keep, w2w[:], "w2q")
+        last.append(gather3(3, P, P))
+        for a in range(2):
+            add_turned(3, a, last[a], 0)
+            words = zt[a][:].rearrange("v u p e -> v (u p e)").bitcast(F32)
+            back = psum.tile([P, 2, P], F32, tag="fin", bufs=3, name="back%d" % a)
+            for u in range(2):
+                nc.tensor.transpose(back[:, u, :], words[:, u * P : (u + 1) * P], ident[:])
+            zw = keep.tile([P, P, PACK], BF16, align_bytes=64, name="zw%d" % a)
+            copy = nc.scalar.copy if a == 0 else nc.vector.tensor_copy
+            copy(
+                out=zw[:].rearrange("p v j -> p (v j)").bitcast(F32).rearrange("p (v u) -> p v u", u=2),
+                in_=back[:].rearrange("p u v -> p v u"),
+            )
+            zq = quantize(nc, keep, zw[:], "zq%d" % a)
+            res = psum.tile([P, 2, P], F32, tag="fin", bufs=3, name="res%d" % a)
+            for c in range(2):
+                mx(nc, res[:, c, :], w2q, slice(c * P, (c + 1) * P), zq)
+            o = keep.tile([P, 2, P], F32, name="o%d" % a)
+            copy(out=o[:], in_=res[:])
+            nc.sync.dma_start(out_v[:, :, a * P : (a + 1) * P], o[:])

@@ -1,7 +1,6 @@
 from contextlib import ExitStack
 
 import concourse.mybir as mybir
-from concourse.masks import make_identity
 
 K, T, S, V, H, N = 512, 1024, 512, 256, 512, 256
 FLOPS = 2 * K * H * S + 2 * H * N * V
@@ -26,9 +25,9 @@ def weave(copy, woven, rows):
     )
 
 
-def quantize(nc, pool, woven, name):
+def quantize(nc, pool, woven, name, tag=""):
     width = woven.shape[1]
-    codes = pool.tile([P, width], U32, align_bytes=64, name=name + "_codes")
+    codes = pool.tile([P, width], U32, align_bytes=64, name=name + "_codes", tag=tag)
     scales = pool.tile([P, width], U8, align_bytes=64, name=name + "_scales")
     nc.vector.quantize_mx(out=codes[:].bitcast(FP8X4), scales=scales[:], in_=woven.rearrange("p w j -> p (w j)"))
     return codes, scales
@@ -54,9 +53,8 @@ def tile_picked_lapl_silu_e_kernel(tc, xT, w1, w2, gate, offs, cen, pos1, pos2, 
         pos2_t = lists.tile([P, V // 16], U16, name="pos2_t")
 
         x_rows = xT.rearrange("(p j) t -> p j t", j=PACK)
-        w1_rows = w1.rearrange("(p j) i -> p j i", j=PACK)
         xp = [keep.tile([P, T], F32, name="xp%d" % j) for j in range(PACK)]
-        w1r = [keep.tile([P, PACK, 256], F32, name="w1r%d" % c) for c in range(2)]
+        w1r = keep.tile([P, PACK, H], F32, name="w1r")
         gate_t = keep.tile([P, 2, V], F32, name="gate_t")
         w2r = keep.tile([P, PACK, N], F32, name="w2r")
 
@@ -64,112 +62,108 @@ def tile_picked_lapl_silu_e_kernel(tc, xT, w1, w2, gate, offs, cen, pos1, pos2, 
         nc.sync.dma_start(offs_t[:], offs)
         for j in range(1, PACK):
             nc.sync.dma_start(xp[j][:], x_rows[:, j, :])
-        nc.sync.dma_start(w1r[0][:], w1_rows[:, :, 0:256])
+        nc.sync.dma_start(w1r[:], w1.rearrange("(p j) i -> p j i", j=PACK))
         nc.sync.dma_start(gate_t[:], gate.rearrange("d p v -> p d v"))
-        nc.sync.dma_start(w1r[1][:], w1_rows[:, :, 256:512])
-        nc.sync.dma_start(cen_t[:], cen)
         nc.sync.dma_start(pos1_t[:], pos1)
         nc.sync.dma_start(pos2_t[:], pos2)
-        nc.sync.dma_start(w2r[:], w2.rearrange("(p j) m -> p j m", j=PACK))
+        nc.sync.dma_start(cen_t[:], cen)
+        w2_rows = w2.rearrange("(g t q) m -> q g t m", t=PACK, q=4)
+        for q in range(4):
+            nc.sync.dma_start(w2r[q:P:4, :, :], w2_rows[q])
 
-        ident = keep.tile([P, P], F32, name="ident")
-        make_identity(nc, ident[:])
         zero_in = keep.tile([P, 1], F32, name="zero_in")
         zero = keep.tile([P, 1], F32, name="zero")
         nc.vector.memset(zero_in[:], 0.0)
         nc.scalar.activation(out=zero[:], in_=zero_in[:], func=ACT.Silu)
 
-        xg = [keep.tile([P, PACK, 256], F32, name="xg%d" % a) for a in range(2)]
+        def woven_tile(width, name, tag=""):
+            return keep.tile([P, width, PACK], BF16, align_bytes=64, name=name, tag=tag)
+
+        def weave_w1(t, tag="", shares=((nc.scalar.copy, 0, 32),)):
+            woven = woven_tile(P, "w1w%d" % t, tag)
+            for copy, lo, hi in shares:
+                copy(
+                    out=woven[:].rearrange("p (g q) j -> p g j q", q=4)[:, lo:hi],
+                    in_=w1r[:].rearrange("p j (g t q) -> p t g j q", t=PACK, q=4)[:, t, lo:hi],
+                )
+            return woven
+
+        xg = [keep.tile([P, PACK, 256], BF16, name="xg%d" % a) for a in range(2)]
+        x2b = keep.tile([P, T], BF16, name="x2b")
+        nc.scalar.copy(out=x2b[:], in_=xp[2][:])
         for j in range(PACK):
             for a in range(2):
-                nc.vector.tensor_copy(out=xg[a][:, j, :], in_=xp[j][:].indirect(offs_t[:, 16 * a : 16 * a + 16]))
+                picks = offs_t[:, 16 * a : 16 * a + 16]
+                if (j, a) == (2, 1):
+                    nc.scalar.activation(out=xg[a][:, j, :], in_=x2b[:].indirect(picks), func=ACT.Copy)
+                else:
+                    nc.vector.tensor_copy(out=xg[a][:, j, :], in_=xp[j][:].indirect(picks))
 
-        w1w = [keep.tile([P, P, PACK], BF16, align_bytes=64, name="w1w%d" % t) for t in range(4)]
-        xw = [keep.tile([P, 256, PACK], BF16, align_bytes=64, name="xw%d" % a) for a in range(2)]
-
-        def w1_cols(t):
-            return w1r[t // 2][:, :, (t % 2) * P : (t % 2 + 1) * P]
-
-        weave(nc.scalar.copy, w1w[0][:], w1_cols(0))
+        xw = [woven_tile(256, "xw%d" % a, "") for a in range(2)]
         weave(nc.scalar.copy, xw[0][:], xg[0][:])
-        w1q = [quantize(nc, keep, w1w[0][:], "w1q0")]
         weave(nc.vector.tensor_copy, xw[1][:], xg[1][:])
-        xq = [None, None]
-        xq[1] = quantize(nc, keep, xw[1][:], "xq1")
-        xq[0] = quantize(nc, keep, xw[0][:], "xq0")
+        xq = [quantize(nc, keep, xw[0][:], "xq0")]
+        xq.append(quantize(nc, keep, xw[1][:], "xq1"))
+        w1q = [quantize(nc, keep, weave_w1(0, "slot_d")[:], "w1q0")]
+        w1w1 = weave_w1(1)
+        w1w2 = weave_w1(2)
+        w1w3 = weave_w1(3, "slot_d", ((nc.vector.tensor_copy, 0, 32),))
+        w1q.append(quantize(nc, keep, w1w1[:], "w1q1", "slot_c"))
+        w1q3 = quantize(nc, keep, w1w3[:], "w1q3")
+        w1q.extend([quantize(nc, keep, w1w2[:], "w1q2"), w1q3])
 
         h = [keep.tile([P, S], F32, name="h%d" % t) for t in range(4)]
         allc = slice(0, P)
-        for a in (1, 0):
-            acc = psum.tile([P, 256], F32, tag="acc", bufs=3, name="acc0_%d" % a)
+        for a in range(2):
+            acc = psum.tile([P, 256], F32, tag="acc", bufs=4, name="acc0_%d" % a)
             mx(nc, acc[:], w1q[0], allc, xq[a])
             nc.scalar.activation(out=h[0][:, 256 * a : 256 * a + 256], in_=acc[:], func=ACT.Silu, bias=zero[:])
 
-        ngate = keep.tile([P, 2, V], F32, name="ngate")
-        nc.vector.tensor_scalar(out=ngate[:], in0=gate_t[:], scalar1=-1.0, scalar2=None, op0=ALU.mult)
-        weave(nc.vector.tensor_copy, w1w[1][:], w1_cols(1))
-        w1q.append(quantize(nc, keep, w1w[1][:], "w1q1"))
-
         def hidden(t):
-            acc = psum.tile([P, 2, 256], F32, tag="acc", bufs=3, name="acc%d" % t)
+            acc = psum.tile([P, 2, 256], F32, tag="acc", bufs=4, name="acc%d" % t)
             for a in range(2):
                 mx(nc, acc[:, a, :], w1q[t], allc, xq[a])
             nc.scalar.activation(out=h[t][:], in_=acc[:].rearrange("p a s -> p (a s)"), func=ACT.Silu, bias=zero[:])
 
-        zt = [keep.tile([P, 2, P, 2], BF16, name="zt%d" % a) for a in range(2)]
-
-        def gather3(t, lo, n):
-            cols = slice(lo // 16, (lo + n) // 16)
-            c = keep.tile([P, n], F32, name="c%d_%d" % (t, lo))
-            d0 = keep.tile([P, n], F32, name="d0%d_%d" % (t, lo))
-            d1 = keep.tile([P, n], F32, name="d1%d_%d" % (t, lo))
-            nc.vector.tensor_copy(out=c[:], in_=h[t][:].indirect(cen_t[:, cols]))
-            nc.vector.tensor_tensor(out=d0[:], in0=h[t][:].indirect(pos1_t[:, cols]), in1=ngate[:, 0, lo : lo + n], op=ALU.mult)
-            nc.vector.tensor_tensor(out=d1[:], in0=h[t][:].indirect(pos2_t[:, cols]), in1=ngate[:, 1, lo : lo + n], op=ALU.mult)
-            return c, d0, d1
-
-        def add_turned(t, a, terms, lo):
-            turned = psum.tile([P, P], F32, tag="turned", bufs=2, name="turned%d_%d" % (t, a))
-            for n, term in enumerate(terms):
-                nc.tensor.matmul(turned[:], term[:, lo : lo + P], ident[:], start=(n == 0), stop=(n == 2), is_transpose=True)
-            nc.scalar.copy(
-                out=zt[a][:, :, 32 * t : 32 * t + 32, :],
-                in_=turned[:].rearrange("v (q u e) -> v u q e", u=2, e=2),
-            )
-
         hidden(1)
-        w2w = keep.tile([P, N, PACK], BF16, align_bytes=64, name="w2w")
-        for t in range(3):
-            terms = gather3(t, 0, V)
-            if t < 2:
-                weave(nc.scalar.copy, w1w[t + 2][:], w1_cols(t + 2))
-                w1q.append(quantize(nc, keep, w1w[t + 2][:], "w1q%d" % (t + 2)))
-                hidden(t + 2)
-            else:
-                weave(nc.scalar.copy, w2w[:], w2r[:])
-            for a in range(2):
-                add_turned(t, a, terms, a * P)
+        hidden(2)
+        hidden(3)
+        w2w = woven_tile(N, "w2w", "slot_c")
+        weave(nc.scalar.copy, w2w[:], w2r[:])
+        w2q = quantize(nc, keep, w2w[:], "w2q")
+
+        own = keep.tile([P, PACK, V], F32, name="own")
+        second = keep.tile([P, PACK, V], F32, name="second")
+        for t in range(4):
+            first = keep.tile([P, V], F32, align_bytes=64, name="first%d" % t)
+            nc.vector.tensor_tensor(out=first[:], in0=h[t][:].indirect(pos1_t[:]), in1=gate_t[:, 0, :], op=ALU.mult)
+            nc.vector.tensor_tensor(out=second[:, t, :], in0=h[t][:].indirect(pos2_t[:]), in1=gate_t[:, 1, :], op=ALU.mult)
+            for lo, n in ((0, V),) if t < 3 else ((0, P), (P, P)):
+                nc.vector.tensor_tensor(
+                    out=own[:, t, lo : lo + n], in0=h[t][:].indirect(cen_t[:, lo // 16 : (lo + n) // 16]),
+                    in1=first[:, lo : lo + n], op=ALU.subtract,
+                )
 
         out_v = out.rearrange("(c p) v -> p c v", p=P)
-        last = [gather3(3, 0, P)]
-        w2q = quantize(nc, keep, w2w[:], "w2q")
-        last.append(gather3(3, P, P))
+        zw = [woven_tile(P, "zw%d" % a) for a in range(2)]
         for a in range(2):
-            add_turned(3, a, last[a], 0)
-            words = zt[a][:].rearrange("v u p e -> v (u p e)").bitcast(F32)
-            back = psum.tile([P, 2, P], F32, tag="fin", bufs=3, name="back%d" % a)
-            for u in range(2):
-                nc.tensor.transpose(back[:, u, :], words[:, u * P : (u + 1) * P], ident[:])
-            zw = keep.tile([P, P, PACK], BF16, align_bytes=64, name="zw%d" % a)
-            copy = nc.scalar.copy if a == 0 else nc.vector.tensor_copy
-            copy(
-                out=zw[:].rearrange("p v j -> p (v j)").bitcast(F32).rearrange("p (v u) -> p v u", u=2),
-                in_=back[:].rearrange("p u v -> p v u"),
+            cols = slice(a * P, (a + 1) * P)
+            nc.vector.tensor_tensor(
+                out=zw[a][:].rearrange("p (c i) j -> p c j i", i=4),
+                in0=own[:, :, cols].rearrange("p j (c i) -> p c j i", i=4),
+                in1=second[:, :, cols].rearrange("p j (c i) -> p c j i", i=4),
+                op=ALU.subtract,
             )
-            zq = quantize(nc, keep, zw[:], "zq%d" % a)
-            res = psum.tile([P, 2, P], F32, tag="fin", bufs=3, name="res%d" % a)
-            for c in range(2):
-                mx(nc, res[:, c, :], w2q, slice(c * P, (c + 1) * P), zq)
-            o = keep.tile([P, 2, P], F32, name="o%d" % a)
-            copy(out=o[:], in_=res[:])
-            nc.sync.dma_start(out_v[:, :, a * P : (a + 1) * P], o[:])
+        zq = [quantize(nc, keep, zw[a][:], "zq%d" % a) for a in range(2)]
+        res = psum.tile([P, 2, P], F32, tag="res", bufs=3, name="res0")
+        for c in range(2):
+            mx(nc, res[:, c, :], w2q, slice(c * P, (c + 1) * P), zq[0])
+        o = keep.tile([P, 2, P], F32, name="o0")
+        nc.scalar.copy(out=o[:], in_=res[:])
+        nc.sync.dma_start(out_v[:, :, 0:P], o[:])
+        o = keep.tile([P, 2, P], F32, name="o1")
+        for c, copy in enumerate((nc.vector.tensor_copy, nc.scalar.copy)):
+            res = psum.tile([P, P], F32, tag="res", bufs=3, name="res1_%d" % c)
+            mx(nc, res[:], w2q, slice(c * P, (c + 1) * P), zq[1])
+            copy(out=o[:, c, :], in_=res[:])
+        nc.sync.dma_start(out_v[:, :, P:V], o[:])

@@ -67,9 +67,9 @@ def tile_picked_lapl_silu_e_kernel(tc, xT, w1, w2, gate, offs, cen, pos1, pos2, 
         nc.sync.dma_start(pos1_t[:], pos1)
         nc.sync.dma_start(pos2_t[:], pos2)
         nc.sync.dma_start(cen_t[:], cen)
-        w2_rows = w2.rearrange("(g t q) m -> q g t m", t=PACK, q=4)
-        for q in range(4):
-            nc.sync.dma_start(w2r[q:P:4, :, :], w2_rows[q])
+        w2_rows = w2.rearrange("(g t q) m -> q g t m", t=PACK, q=2)
+        for q in range(2):
+            nc.sync.dma_start(w2r[q:P:2, :, :], w2_rows[q])
 
         zero_in = keep.tile([P, 1], F32, name="zero_in")
         zero = keep.tile([P, 1], F32, name="zero")
@@ -79,12 +79,12 @@ def tile_picked_lapl_silu_e_kernel(tc, xT, w1, w2, gate, offs, cen, pos1, pos2, 
         def woven_tile(width, name, tag=""):
             return keep.tile([P, width, PACK], BF16, align_bytes=64, name=name, tag=tag)
 
-        def weave_w1(t, tag="", shares=((nc.scalar.copy, 0, 32),)):
+        def weave_w1(t, tag="", shares=((nc.scalar.copy, 0, 64),)):
             woven = woven_tile(P, "w1w%d" % t, tag)
             for copy, lo, hi in shares:
                 copy(
-                    out=woven[:].rearrange("p (g q) j -> p g j q", q=4)[:, lo:hi],
-                    in_=w1r[:].rearrange("p j (g t q) -> p t g j q", t=PACK, q=4)[:, t, lo:hi],
+                    out=woven[:].rearrange("p (g q) j -> p g j q", q=2)[:, lo:hi],
+                    in_=w1r[:].rearrange("p j (g t q) -> p t g j q", t=PACK, q=2)[:, t, lo:hi],
                 )
             return woven
 
@@ -107,7 +107,7 @@ def tile_picked_lapl_silu_e_kernel(tc, xT, w1, w2, gate, offs, cen, pos1, pos2, 
         w1q = [quantize(nc, keep, weave_w1(0, "slot_d")[:], "w1q0")]
         w1w1 = weave_w1(1)
         w1w2 = weave_w1(2)
-        w1w3 = weave_w1(3, "slot_d", ((nc.vector.tensor_copy, 0, 32),))
+        w1w3 = weave_w1(3, "slot_d", ((nc.vector.tensor_copy, 0, 64),))
         w1q.append(quantize(nc, keep, w1w1[:], "w1q1", "slot_c"))
         w1q3 = quantize(nc, keep, w1w3[:], "w1q3")
         w1q.extend([quantize(nc, keep, w1w2[:], "w1q2"), w1q3])
@@ -155,15 +155,10 @@ def tile_picked_lapl_silu_e_kernel(tc, xT, w1, w2, gate, offs, cen, pos1, pos2, 
                 op=ALU.subtract,
             )
         zq = [quantize(nc, keep, zw[a][:], "zq%d" % a) for a in range(2)]
-        res = psum.tile([P, 2, P], F32, tag="res", bufs=3, name="res0")
-        for c in range(2):
-            mx(nc, res[:, c, :], w2q, slice(c * P, (c + 1) * P), zq[0])
-        o = keep.tile([P, 2, P], F32, name="o0")
-        nc.scalar.copy(out=o[:], in_=res[:])
-        nc.sync.dma_start(out_v[:, :, 0:P], o[:])
-        o = keep.tile([P, 2, P], F32, name="o1")
-        for c, copy in enumerate((nc.vector.tensor_copy, nc.scalar.copy)):
-            res = psum.tile([P, P], F32, tag="res", bufs=3, name="res1_%d" % c)
-            mx(nc, res[:], w2q, slice(c * P, (c + 1) * P), zq[1])
-            copy(out=o[:, c, :], in_=res[:])
-        nc.sync.dma_start(out_v[:, :, P:V], o[:])
+        for a in range(2):
+            o = keep.tile([P, 2, P], F32, name="o%d" % a)
+            for c, copy in enumerate((nc.scalar.copy, nc.vector.tensor_copy)):
+                res = psum.tile([P, P], F32, tag="res", bufs=4, name="res%d_%d" % (a, c))
+                mx(nc, res[:], w2q, slice(c * P, (c + 1) * P), zq[a])
+                copy(out=o[:, c, :], in_=res[:])
+            nc.sync.dma_start(out_v[:, :, a * P : (a + 1) * P], o[:])

@@ -16,6 +16,8 @@ ALU = mybir.AluOpType
 
 P = 128
 PACK = 4
+HALF = S // 2
+W1_VECTOR_SHARE = 88
 
 
 def weave(copy, woven, rows):
@@ -25,9 +27,9 @@ def weave(copy, woven, rows):
     )
 
 
-def quantize(nc, pool, woven, name, tag=""):
+def quantize(nc, pool, woven, name):
     width = woven.shape[1]
-    codes = pool.tile([P, width], U32, align_bytes=64, name=name + "_codes", tag=tag)
+    codes = pool.tile([P, width], U32, align_bytes=64, name=name + "_codes")
     scales = pool.tile([P, width], U8, align_bytes=64, name=name + "_scales")
     nc.vector.quantize_mx(out=codes[:].bitcast(FP8X4), scales=scales[:], in_=woven.rearrange("p w j -> p (w j)"))
     return codes, scales
@@ -49,100 +51,97 @@ def tile_picked_lapl_silu_e_kernel(tc, xT, w1, w2, gate, offs, cen, pos1, pos2, 
 
         offs_t = lists.tile([P, S // 16], U16, name="offs_t")
         cen_t = lists.tile([P, V // 16], U16, name="cen_t")
-        pos1_t = lists.tile([P, V // 16], U16, name="pos1_t")
-        pos2_t = lists.tile([P, V // 16], U16, name="pos2_t")
+        pos_t = [lists.tile([P, V // 16], U16, name="pos%d_t" % d) for d in range(2)]
 
         x_rows = xT.rearrange("(p j) t -> p j t", j=PACK)
         xp = [keep.tile([P, T], F32, name="xp%d" % j) for j in range(PACK)]
         w1r = keep.tile([P, PACK, H], F32, name="w1r")
-        gate_t = keep.tile([P, 2, V], F32, name="gate_t")
         w2r = keep.tile([P, PACK, N], F32, name="w2r")
+        gate_t = keep.tile([P, 2, V], F32, name="gate_t")
 
         nc.sync.dma_start(xp[0][:], x_rows[:, 0, :])
         nc.sync.dma_start(offs_t[:], offs)
         for j in range(1, PACK):
             nc.sync.dma_start(xp[j][:], x_rows[:, j, :])
         nc.sync.dma_start(w1r[:], w1.rearrange("(p j) i -> p j i", j=PACK))
+        nc.sync.dma_start(w2r[:], w2.rearrange("(p j) m -> p j m", j=PACK))
         nc.sync.dma_start(gate_t[:], gate.rearrange("d p v -> p d v"))
-        nc.sync.dma_start(pos1_t[:], pos1)
-        nc.sync.dma_start(pos2_t[:], pos2)
+        nc.sync.dma_start(pos_t[0][:], pos1)
+        nc.sync.dma_start(pos_t[1][:], pos2)
         nc.sync.dma_start(cen_t[:], cen)
-        w2_rows = w2.rearrange("(g t q) m -> q g t m", t=PACK, q=2)
-        for q in range(2):
-            nc.sync.dma_start(w2r[q:P:2, :, :], w2_rows[q])
 
         zero_in = keep.tile([P, 1], F32, name="zero_in")
         zero = keep.tile([P, 1], F32, name="zero")
         nc.vector.memset(zero_in[:], 0.0)
         nc.scalar.activation(out=zero[:], in_=zero_in[:], func=ACT.Silu)
 
-        def woven_tile(width, name, tag=""):
-            return keep.tile([P, width, PACK], BF16, align_bytes=64, name=name, tag=tag)
+        def woven_tile(width, name):
+            return keep.tile([P, width, PACK], BF16, align_bytes=64, name=name)
 
-        def weave_w1(t, tag="", shares=((nc.scalar.copy, 0, 64),)):
-            woven = woven_tile(P, "w1w%d" % t, tag)
-            for copy, lo, hi in shares:
-                copy(
-                    out=woven[:].rearrange("p (g q) j -> p g j q", q=2)[:, lo:hi],
-                    in_=w1r[:].rearrange("p j (g t q) -> p t g j q", t=PACK, q=2)[:, t, lo:hi],
-                )
-            return woven
+        def scalar_gather(out, in_):
+            nc.scalar.activation(out=out, in_=in_, func=ACT.Copy)
 
-        xg = [keep.tile([P, PACK, 256], BF16, name="xg%d" % a) for a in range(2)]
-        x2b = keep.tile([P, T], BF16, name="x2b")
-        nc.scalar.copy(out=x2b[:], in_=xp[2][:])
+        xg = [keep.tile([P, PACK, HALF], BF16, name="xg%d" % a) for a in range(2)]
         for j in range(PACK):
-            for a in range(2):
-                picks = offs_t[:, 16 * a : 16 * a + 16]
-                if (j, a) == (2, 1):
-                    nc.scalar.activation(out=xg[a][:, j, :], in_=x2b[:].indirect(picks), func=ACT.Copy)
-                else:
-                    nc.vector.tensor_copy(out=xg[a][:, j, :], in_=xp[j][:].indirect(picks))
+            for a, gather in enumerate((nc.vector.tensor_copy, scalar_gather)):
+                gather(out=xg[a][:, j, :], in_=xp[j][:].indirect(offs_t[:, 16 * a : 16 * a + 16]))
+        xw = [woven_tile(HALF, "xw%d" % a) for a in range(2)]
+        weave(nc.vector.tensor_copy, xw[0][:], xg[0][:])
+        weave(nc.scalar.copy, xw[1][:], xg[1][:])
+        xq = [quantize(nc, keep, xw[a][:], "xq%d" % a) for a in range(2)]
 
-        xw = [woven_tile(256, "xw%d" % a, "") for a in range(2)]
-        weave(nc.scalar.copy, xw[0][:], xg[0][:])
-        weave(nc.vector.tensor_copy, xw[1][:], xg[1][:])
-        xq = [quantize(nc, keep, xw[0][:], "xq0")]
-        xq.append(quantize(nc, keep, xw[1][:], "xq1"))
-        w1q = [quantize(nc, keep, weave_w1(0, "slot_d")[:], "w1q0")]
-        w1w1 = weave_w1(1)
-        w1w2 = weave_w1(2)
-        w1w3 = weave_w1(3, "slot_d", ((nc.vector.tensor_copy, 0, 64),))
-        w1q.append(quantize(nc, keep, w1w1[:], "w1q1", "slot_c"))
-        w1q3 = quantize(nc, keep, w1w3[:], "w1q3")
-        w1q.extend([quantize(nc, keep, w1w2[:], "w1q2"), w1q3])
+        w1_cols = w1r[:].rearrange("p j (m t) -> p m j t", t=PACK)
+        w1w = [keep.tile([P, 2, P, PACK], BF16, align_bytes=64, name="w1w%d" % u) for u in range(2)]
 
-        h = [keep.tile([P, S], F32, name="h%d" % t) for t in range(4)]
+        def weave_w1(copy, u, lo, hi):
+            copy(out=w1w[u][:].rearrange("p t m j -> p m j t")[:, lo:hi], in_=w1_cols[:, lo:hi, :, 2 * u : 2 * u + 2])
+
+        weave_w1(nc.vector.tensor_copy, 0, 0, W1_VECTOR_SHARE)
+        weave_w1(nc.scalar.copy, 0, W1_VECTOR_SHARE, P)
+        w1q = [quantize(nc, keep, w1w[0][:, t], "w1q%d" % t) for t in range(2)]
+        weave_w1(nc.scalar.copy, 1, 0, P)
+        w1q.extend(quantize(nc, keep, w1w[1][:, t], "w1q%d" % (2 + t)) for t in range(2))
+
+        w2w = woven_tile(N, "w2w")
+        weave(nc.vector.tensor_copy, w2w[:], w2r[:])
+        w2q = quantize(nc, keep, w2w[:], "w2q")
+
+        h = [keep.tile([P, S], F32, name="h%d" % t) for t in range(PACK)]
         allc = slice(0, P)
         for a in range(2):
-            acc = psum.tile([P, 256], F32, tag="acc", bufs=4, name="acc0_%d" % a)
+            acc = psum.tile([P, HALF], F32, tag="acc", bufs=4, name="acc0_%d" % a)
             mx(nc, acc[:], w1q[0], allc, xq[a])
-            nc.scalar.activation(out=h[0][:, 256 * a : 256 * a + 256], in_=acc[:], func=ACT.Silu, bias=zero[:])
-
-        def hidden(t):
-            acc = psum.tile([P, 2, 256], F32, tag="acc", bufs=4, name="acc%d" % t)
+            nc.scalar.activation(out=h[0][:, HALF * a : HALF * (a + 1)], in_=acc[:], func=ACT.Silu, bias=zero[:])
+        for t in range(1, PACK):
+            acc = psum.tile([P, 2, HALF], F32, tag="acc", bufs=4, name="acc%d" % t)
             for a in range(2):
                 mx(nc, acc[:, a, :], w1q[t], allc, xq[a])
             nc.scalar.activation(out=h[t][:], in_=acc[:].rearrange("p a s -> p (a s)"), func=ACT.Silu, bias=zero[:])
 
-        hidden(1)
-        hidden(2)
-        hidden(3)
-        w2w = woven_tile(N, "w2w", "slot_c")
-        weave(nc.scalar.copy, w2w[:], w2r[:])
-        w2q = quantize(nc, keep, w2w[:], "w2q")
-
+        last = PACK - 1
+        fetched = keep.tile([P, 2, V], F32, name="fetched")
         own = keep.tile([P, PACK, V], F32, name="own")
-        second = keep.tile([P, PACK, V], F32, name="second")
-        for t in range(4):
-            first = keep.tile([P, V], F32, align_bytes=64, name="first%d" % t)
-            nc.vector.tensor_tensor(out=first[:], in0=h[t][:].indirect(pos1_t[:]), in1=gate_t[:, 0, :], op=ALU.mult)
-            nc.vector.tensor_tensor(out=second[:, t, :], in0=h[t][:].indirect(pos2_t[:]), in1=gate_t[:, 1, :], op=ALU.mult)
-            for lo, n in ((0, V),) if t < 3 else ((0, P), (P, P)):
-                nc.vector.tensor_tensor(
-                    out=own[:, t, lo : lo + n], in0=h[t][:].indirect(cen_t[:, lo // 16 : (lo + n) // 16]),
-                    in1=first[:, lo : lo + n], op=ALU.subtract,
-                )
+        for d in range(2):
+            scalar_gather(out=fetched[:, d, :], in_=h[last][:].indirect(pos_t[d][:]))
+        for t in range(PACK):
+            scalar_gather(out=own[:, t, :], in_=h[t][:].indirect(cen_t[:]))
+
+        prod = keep.tile([P, PACK, 2, V], F32, name="prod")
+        pull = keep.tile([P, PACK, V], F32, name="pull")
+
+        def weighted(t, d):
+            nc.vector.tensor_tensor(out=prod[:, t, d, :], in0=h[t][:].indirect(pos_t[d][:]), in1=gate_t[:, d, :], op=ALU.mult)
+
+        def add_pair(tiles, cols):
+            nc.vector.tensor_tensor(out=pull[:, tiles, cols], in0=prod[:, tiles, 0, cols], in1=prod[:, tiles, 1, cols], op=ALU.add)
+
+        for t, d in ((0, 0), (0, 1), (1, 0), (1, 1), (2, 0)):
+            weighted(t, d)
+        nc.vector.tensor_tensor(out=prod[:, last], in0=fetched[:], in1=gate_t[:], op=ALU.mult)
+        weighted(2, 1)
+        add_pair(slice(0, 2), slice(0, V))
+        for a in range(2):
+            add_pair(slice(2, 4), slice(a * P, (a + 1) * P))
 
         out_v = out.rearrange("(c p) v -> p c v", p=P)
         zw = [woven_tile(P, "zw%d" % a) for a in range(2)]
@@ -151,7 +150,7 @@ def tile_picked_lapl_silu_e_kernel(tc, xT, w1, w2, gate, offs, cen, pos1, pos2, 
             nc.vector.tensor_tensor(
                 out=zw[a][:].rearrange("p (c i) j -> p c j i", i=4),
                 in0=own[:, :, cols].rearrange("p j (c i) -> p c j i", i=4),
-                in1=second[:, :, cols].rearrange("p j (c i) -> p c j i", i=4),
+                in1=pull[:, :, cols].rearrange("p j (c i) -> p c j i", i=4),
                 op=ALU.subtract,
             )
         zq = [quantize(nc, keep, zw[a][:], "zq%d" % a) for a in range(2)]

@@ -84,11 +84,23 @@ def tile_picked_lapl_silu_e_kernel(tc, xT, w1, w2, gate, offs, cen, pos1, pos2, 
         xg = [keep.tile([P, PACK, HALF], BF16, name="xg%d" % a) for a in range(2)]
         for j in range(PACK):
             for a, gather in enumerate((nc.vector.tensor_copy, scalar_gather)):
-                gather(out=xg[a][:, j, :], in_=xp[j][:].indirect(offs_t[:, 16 * a : 16 * a + 16]))
+                for lo, n in ((0, HALF),) if j < PACK - 1 else ((0, P), (P, P)):
+                    first = (HALF * a + lo) // 16
+                    gather(out=xg[a][:, j, lo : lo + n], in_=xp[j][:].indirect(offs_t[:, first : first + n // 16]))
         xw = [woven_tile(HALF, "xw%d" % a) for a in range(2)]
-        weave(nc.vector.tensor_copy, xw[0][:], xg[0][:])
-        weave(nc.scalar.copy, xw[1][:], xg[1][:])
-        xq = [quantize(nc, keep, xw[a][:], "xq%d" % a) for a in range(2)]
+        xq = []
+        for a, copy in enumerate((nc.vector.tensor_copy, nc.scalar.copy)):
+            codes = keep.tile([P, HALF], U32, align_bytes=64, name="xq%d_codes" % a)
+            scales = keep.tile([P, HALF], U8, align_bytes=64, name="xq%d_scales" % a)
+            xq.append((codes, scales))
+            for lo in (0, P):
+                weave(copy, xw[a][:, lo : lo + P], xg[a][:, :, lo : lo + P])
+        for a in range(2):
+            for lo in (0, P):
+                nc.vector.quantize_mx(
+                    out=xq[a][0][:, lo : lo + P].bitcast(FP8X4), scales=xq[a][1][:, lo : lo + P],
+                    in_=xw[a][:, lo : lo + P].rearrange("p w j -> p (w j)"),
+                )
 
         w1_cols = w1r[:].rearrange("p j (m t) -> p m j t", t=PACK)
         w1w = [keep.tile([P, 2, P, PACK], BF16, align_bytes=64, name="w1w%d" % u) for u in range(2)]
@@ -123,8 +135,11 @@ def tile_picked_lapl_silu_e_kernel(tc, xT, w1, w2, gate, offs, cen, pos1, pos2, 
         own = keep.tile([P, PACK, V], F32, name="own")
         for d in range(2):
             scalar_gather(out=fetched[:, d, :], in_=h[last][:].indirect(pos_t[d][:]))
-        for t in range(PACK):
+        for t in range(2):
             scalar_gather(out=own[:, t, :], in_=h[t][:].indirect(cen_t[:]))
+        for lo in (0, P):
+            for t in range(2, PACK):
+                scalar_gather(out=own[:, t, lo : lo + P], in_=h[t][:].indirect(cen_t[:, lo // 16 : (lo + P) // 16]))
 
         prod = keep.tile([P, PACK, 2, V], F32, name="prod")
         pull = keep.tile([P, PACK, V], F32, name="pull")
@@ -135,11 +150,13 @@ def tile_picked_lapl_silu_e_kernel(tc, xT, w1, w2, gate, offs, cen, pos1, pos2, 
         def add_pair(tiles, cols):
             nc.vector.tensor_tensor(out=pull[:, tiles, cols], in0=prod[:, tiles, 0, cols], in1=prod[:, tiles, 1, cols], op=ALU.add)
 
-        for t, d in ((0, 0), (0, 1), (1, 0), (1, 1), (2, 0)):
-            weighted(t, d)
-        nc.vector.tensor_tensor(out=prod[:, last], in0=fetched[:], in1=gate_t[:], op=ALU.mult)
-        weighted(2, 1)
+        for t in range(last):
+            for d in range(2):
+                weighted(t, d)
         add_pair(slice(0, 2), slice(0, V))
+        for a in range(2):
+            cols = slice(a * P, (a + 1) * P)
+            nc.vector.tensor_tensor(out=prod[:, last, :, cols], in0=fetched[:, :, cols], in1=gate_t[:, :, cols], op=ALU.mult)
         for a in range(2):
             add_pair(slice(2, 4), slice(a * P, (a + 1) * P))
 

@@ -27,9 +27,9 @@ def weave(copy, woven, rows):
     )
 
 
-def quantize(nc, pool, woven, name):
+def quantize(nc, pool, woven, name, tag=""):
     width = woven.shape[1]
-    codes = pool.tile([P, width], U32, align_bytes=64, name=name + "_codes")
+    codes = pool.tile([P, width], U32, align_bytes=64, name=name + "_codes", tag=tag)
     scales = pool.tile([P, width], U8, align_bytes=64, name=name + "_scales")
     nc.vector.quantize_mx(out=codes[:].bitcast(FP8X4), scales=scales[:], in_=woven.rearrange("p w j -> p (w j)"))
     return codes, scales
@@ -54,7 +54,7 @@ def tile_picked_lapl_silu_e_kernel(tc, xT, w1, w2, gate, offs, cen, pos1, pos2, 
         pos_t = [lists.tile([P, V // 16], U16, name="pos%d_t" % d) for d in range(2)]
 
         x_rows = xT.rearrange("(p j) t -> p j t", j=PACK)
-        xp = [keep.tile([P, T], F32, name="xp%d" % j) for j in range(PACK)]
+        xp = [keep.tile([P, T], F32, align_bytes=64, name="xp%d" % j, tag="xp%d" % j) for j in range(PACK)]
         w1r = keep.tile([P, PACK, H], F32, name="w1r")
         w2r = keep.tile([P, PACK, N], F32, name="w2r")
         gate_t = keep.tile([P, 2, V], F32, name="gate_t")
@@ -81,26 +81,16 @@ def tile_picked_lapl_silu_e_kernel(tc, xT, w1, w2, gate, offs, cen, pos1, pos2, 
         def scalar_gather(out, in_):
             nc.scalar.activation(out=out, in_=in_, func=ACT.Copy)
 
-        xg = [keep.tile([P, PACK, HALF], BF16, name="xg%d" % a) for a in range(2)]
-        for j in range(PACK):
-            for a, gather in enumerate((nc.vector.tensor_copy, scalar_gather)):
-                for lo, n in ((0, HALF),) if j < PACK - 1 else ((0, P), (P, P)):
-                    first = (HALF * a + lo) // 16
-                    gather(out=xg[a][:, j, lo : lo + n], in_=xp[j][:].indirect(offs_t[:, first : first + n // 16]))
         xw = [woven_tile(HALF, "xw%d" % a) for a in range(2)]
-        xq = []
-        for a, copy in enumerate((nc.vector.tensor_copy, nc.scalar.copy)):
-            codes = keep.tile([P, HALF], U32, align_bytes=64, name="xq%d_codes" % a)
-            scales = keep.tile([P, HALF], U8, align_bytes=64, name="xq%d_scales" % a)
-            xq.append((codes, scales))
-            for lo in (0, P):
-                weave(copy, xw[a][:, lo : lo + P], xg[a][:, :, lo : lo + P])
-        for a in range(2):
-            for lo in (0, P):
-                nc.vector.quantize_mx(
-                    out=xq[a][0][:, lo : lo + P].bitcast(FP8X4), scales=xq[a][1][:, lo : lo + P],
-                    in_=xw[a][:, lo : lo + P].rearrange("p w j -> p (w j)"),
-                )
+        xg = keep.tile([P, PACK, HALF], BF16, name="xg")
+        for j in range(PACK):
+            nc.vector.tensor_copy(out=xw[0][:, :, j], in_=xp[j][:].indirect(offs_t[:, 0 : HALF // 16]))
+            for lo, n in ((0, HALF),) if j < PACK - 1 else ((0, P), (P, P)):
+                first = (HALF + lo) // 16
+                scalar_gather(out=xg[:, j, lo : lo + n], in_=xp[j][:].indirect(offs_t[:, first : first + n // 16]))
+        weave(nc.scalar.copy, xw[1][:, 0:P], xg[:, :, 0:P])
+        weave(nc.vector.tensor_copy, xw[1][:, P:HALF], xg[:, :, P:HALF])
+        xq = [quantize(nc, keep, xw[0][:], "xq0", "xp3"), quantize(nc, keep, xw[1][:], "xq1")]
 
         w1_cols = w1r[:].rearrange("p j (m t) -> p m j t", t=PACK)
         w1w = [keep.tile([P, 2, P, PACK], BF16, align_bytes=64, name="w1w%d" % u) for u in range(2)]
@@ -111,7 +101,8 @@ def tile_picked_lapl_silu_e_kernel(tc, xT, w1, w2, gate, offs, cen, pos1, pos2, 
         weave_w1(nc.vector.tensor_copy, 0, 0, W1_VECTOR_SHARE)
         weave_w1(nc.scalar.copy, 0, W1_VECTOR_SHARE, P)
         w1q = [quantize(nc, keep, w1w[0][:, t], "w1q%d" % t) for t in range(2)]
-        weave_w1(nc.scalar.copy, 1, 0, P)
+        weave_w1(nc.vector.tensor_copy, 1, 0, P - W1_VECTOR_SHARE)
+        weave_w1(nc.scalar.copy, 1, P - W1_VECTOR_SHARE, P)
         w1q.extend(quantize(nc, keep, w1w[1][:, t], "w1q%d" % (2 + t)) for t in range(2))
 
         w2w = woven_tile(N, "w2w")

@@ -124,6 +124,8 @@ def tile_picked_lapl_silu_e_kernel(tc, xT, w1, w2, gate, offs, cen, pos1, pos2, 
         last = PACK - 1
         fetched = keep.tile([P, 2, V], F32, name="fetched")
         own = keep.tile([P, PACK, V], F32, name="own")
+        fetched2 = keep.tile([P, P], F32, name="fetched2")
+        scalar_gather(out=fetched2[:], in_=h[2][:].indirect(pos_t[1][:, P // 16 :]))
         for d in range(2):
             scalar_gather(out=fetched[:, d, :], in_=h[last][:].indirect(pos_t[d][:]))
         for t in range(2):
@@ -141,10 +143,11 @@ def tile_picked_lapl_silu_e_kernel(tc, xT, w1, w2, gate, offs, cen, pos1, pos2, 
         def add_pair(tiles, cols):
             nc.vector.tensor_tensor(out=pull[:, tiles, cols], in0=prod[:, tiles, 0, cols], in1=prod[:, tiles, 1, cols], op=ALU.add)
 
-        for t in range(last):
-            for d in range(2):
-                weighted(t, d)
+        for t, d in ((0, 0), (0, 1), (1, 0), (1, 1), (2, 0)):
+            weighted(t, d)
+        nc.vector.tensor_tensor(out=prod[:, 2, 1, 0:P], in0=h[2][:].indirect(pos_t[1][:, 0 : P // 16]), in1=gate_t[:, 1, 0:P], op=ALU.mult)
         add_pair(slice(0, 2), slice(0, V))
+        nc.vector.tensor_tensor(out=prod[:, 2, 1, P:V], in0=fetched2[:], in1=gate_t[:, 1, P:V], op=ALU.mult)
         for a in range(2):
             cols = slice(a * P, (a + 1) * P)
             nc.vector.tensor_tensor(out=prod[:, last, :, cols], in0=fetched[:, :, cols], in1=gate_t[:, :, cols], op=ALU.mult)
@@ -153,19 +156,36 @@ def tile_picked_lapl_silu_e_kernel(tc, xT, w1, w2, gate, offs, cen, pos1, pos2, 
 
         out_v = out.rearrange("(c p) v -> p c v", p=P)
         zw = [woven_tile(P, "zw%d" % a) for a in range(2)]
-        for a in range(2):
-            cols = slice(a * P, (a + 1) * P)
+
+        def subtract(a, lo, n):
+            cols = slice(a * P + lo, a * P + lo + n)
             nc.vector.tensor_tensor(
-                out=zw[a][:].rearrange("p (c i) j -> p c j i", i=4),
+                out=zw[a][:, lo : lo + n].rearrange("p (c i) j -> p c j i", i=4),
                 in0=own[:, :, cols].rearrange("p j (c i) -> p c j i", i=4),
                 in1=pull[:, :, cols].rearrange("p j (c i) -> p c j i", i=4),
                 op=ALU.subtract,
             )
-        zq = [quantize(nc, keep, zw[a][:], "zq%d" % a) for a in range(2)]
+
+        subtract(0, 0, P)
+        subtract(1, 0, P // 2)
+        zq = [quantize(nc, keep, zw[0][:], "zq0")]
+        subtract(1, P // 2, P // 2)
+        codes = keep.tile([P, P], U32, align_bytes=64, name="zq1_codes")
+        scales = keep.tile([P, P], U8, align_bytes=64, name="zq1_scales")
+        zq.append((codes, scales))
+        for lo in (0, P // 2):
+            piece = slice(lo, lo + P // 2)
+            nc.vector.quantize_mx(
+                out=codes[:, piece].bitcast(FP8X4), scales=scales[:, piece],
+                in_=zw[1][:, piece].rearrange("p w j -> p (w j)"),
+            )
         for a in range(2):
             o = keep.tile([P, 2, P], F32, name="o%d" % a)
-            for c, copy in enumerate((nc.scalar.copy, nc.vector.tensor_copy)):
+            for c, copy in enumerate((nc.scalar.copy, nc.vector.tensor_copy if a else nc.scalar.copy)):
                 res = psum.tile([P, P], F32, tag="res", bufs=4, name="res%d_%d" % (a, c))
                 mx(nc, res[:], w2q, slice(c * P, (c + 1) * P), zq[a])
                 copy(out=o[:, c, :], in_=res[:])
-            nc.sync.dma_start(out_v[:, :, a * P : (a + 1) * P], o[:])
+                if a:
+                    (nc.scalar, nc.sync)[c].dma_start(out_v[:, c, P:V], o[:, c, :])
+            if not a:
+                nc.sync.dma_start(out_v[:, :, 0:P], o[:])

@@ -186,6 +186,6 @@ def tile_picked_lapl_silu_e_kernel(tc, xT, w1, w2, gate, offs, cen, pos1, pos2, 
                 mx(nc, res[:], w2q, slice(c * P, (c + 1) * P), zq[a])
                 copy(out=o[:, c, :], in_=res[:])
                 if a:
-                    (nc.scalar, nc.sync)[c].dma_start(out_v[:, c, P:V], o[:, c, :])
+                    nc.sync.dma_start(out_v[:, c, P:V], o[:, c, :])
             if not a:
                 nc.sync.dma_start(out_v[:, :, 0:P], o[:])

@@ -72,7 +72,7 @@ def tile_picked_lapl_silu_e_kernel(tc, xT, w1, w2, gate, offs, cen, pos1, pos2, 
 
         zero_in = keep.tile([P, 1], F32, name="zero_in")
         zero = keep.tile([P, 1], F32, name="zero")
-        nc.vector.memset(zero_in[:], 0.0)
+        nc.gpsimd.memset(zero_in[:], 0.0)
         nc.scalar.activation(out=zero[:], in_=zero_in[:], func=ACT.Silu)
 
         def woven_tile(width, name):

@@ -18,6 +18,7 @@ P = 128
 PACK = 4
 HALF = S // 2
 W1_VECTOR_SHARE = 88
+FUSED_TARGETS = 64
 
 
 def weave(copy, woven, rows):
@@ -114,25 +115,23 @@ def tile_picked_lapl_silu_e_kernel(tc, xT, w1, w2, gate, offs, cen, pos1, pos2, 
         for a in range(2):
             acc = psum.tile([P, HALF], F32, tag="acc", bufs=4, name="acc0_%d" % a)
             mx(nc, acc[:], w1q[0], allc, xq[a])
-            nc.scalar.activation(out=h[0][:, HALF * a : HALF * (a + 1)], in_=acc[:], func=ACT.Silu, bias=zero[:])
+            nc.scalar.activation(out=h[0][:, HALF * a : HALF * (a + 1)], in_=acc[:], func=ACT.Silu, bias=0.0 if a else zero[:])
         for t in range(1, PACK):
             acc = psum.tile([P, 2, HALF], F32, tag="acc", bufs=4, name="acc%d" % t)
             for a in range(2):
                 mx(nc, acc[:, a, :], w1q[t], allc, xq[a])
-            nc.scalar.activation(out=h[t][:], in_=acc[:].rearrange("p a s -> p (a s)"), func=ACT.Silu, bias=zero[:])
+            nc.scalar.activation(out=h[t][:], in_=acc[:].rearrange("p a s -> p (a s)"), func=ACT.Silu)
 
         last = PACK - 1
         fetched = keep.tile([P, 2, V], F32, name="fetched")
         own = keep.tile([P, PACK, V], F32, name="own")
-        fetched2 = keep.tile([P, P], F32, name="fetched2")
-        scalar_gather(out=fetched2[:], in_=h[2][:].indirect(pos_t[1][:, P // 16 :]))
+        fetched2 = keep.tile([P, V - FUSED_TARGETS], F32, name="fetched2")
+        scalar_gather(out=fetched2[:], in_=h[2][:].indirect(pos_t[1][:, FUSED_TARGETS // 16 :]))
         for d in range(2):
             scalar_gather(out=fetched[:, d, :], in_=h[last][:].indirect(pos_t[d][:]))
-        for t in range(2):
-            scalar_gather(out=own[:, t, :], in_=h[t][:].indirect(cen_t[:]))
-        for lo in (0, P):
-            for t in range(2, PACK):
-                scalar_gather(out=own[:, t, lo : lo + P], in_=h[t][:].indirect(cen_t[:, lo // 16 : (lo + P) // 16]))
+        for lo, n, tiles in ((0, V, (0,)), (0, P, (1, 2, 3)), (P, P, (1,)), (P, P // 2, (2, 3)), (P + P // 2, P // 2, (2, 3))):
+            for t in tiles:
+                scalar_gather(out=own[:, t, lo : lo + n], in_=h[t][:].indirect(cen_t[:, lo // 16 : (lo + n) // 16]))
 
         prod = keep.tile([P, PACK, 2, V], F32, name="prod")
         pull = keep.tile([P, PACK, V], F32, name="pull")
@@ -145,9 +144,12 @@ def tile_picked_lapl_silu_e_kernel(tc, xT, w1, w2, gate, offs, cen, pos1, pos2, 
 
         for t, d in ((0, 0), (0, 1), (1, 0), (1, 1), (2, 0)):
             weighted(t, d)
-        nc.vector.tensor_tensor(out=prod[:, 2, 1, 0:P], in0=h[2][:].indirect(pos_t[1][:, 0 : P // 16]), in1=gate_t[:, 1, 0:P], op=ALU.mult)
+        nc.vector.tensor_tensor(
+            out=prod[:, 2, 1, 0:FUSED_TARGETS], in0=h[2][:].indirect(pos_t[1][:, 0 : FUSED_TARGETS // 16]),
+            in1=gate_t[:, 1, 0:FUSED_TARGETS], op=ALU.mult,
+        )
         add_pair(slice(0, 2), slice(0, V))
-        nc.vector.tensor_tensor(out=prod[:, 2, 1, P:V], in0=fetched2[:], in1=gate_t[:, 1, P:V], op=ALU.mult)
+        nc.vector.tensor_tensor(out=prod[:, 2, 1, FUSED_TARGETS:V], in0=fetched2[:], in1=gate_t[:, 1, FUSED_TARGETS:V], op=ALU.mult)
         for a in range(2):
             cols = slice(a * P, (a + 1) * P)
             nc.vector.tensor_tensor(out=prod[:, last, :, cols], in0=fetched[:, :, cols], in1=gate_t[:, :, cols], op=ALU.mult)

@@ -72,7 +72,7 @@ def tile_picked_lapl_silu_e_kernel(tc, xT, w1, w2, gate, offs, cen, pos1, pos2, 
         nc.sync.dma_start(cen_t[:], cen)
 
         zero_in = keep.tile([P, 1], F32, name="zero_in")
-        zero = keep.tile([P, 1], F32, name="zero")
+        zero = keep.tile([P, 1], F32, name="zero", tag="zero")
         nc.gpsimd.memset(zero_in[:], 0.0)
         nc.scalar.activation(out=zero[:], in_=zero_in[:], func=ACT.Silu)
 
@@ -104,7 +104,8 @@ def tile_picked_lapl_silu_e_kernel(tc, xT, w1, w2, gate, offs, cen, pos1, pos2, 
         w1q = [quantize(nc, keep, w1w[0][:, t], "w1q%d" % t) for t in range(2)]
         weave_w1(nc.vector.tensor_copy, 1, 0, P - W1_VECTOR_SHARE)
         weave_w1(nc.scalar.copy, 1, P - W1_VECTOR_SHARE, P)
-        w1q.extend(quantize(nc, keep, w1w[1][:, t], "w1q%d" % (2 + t)) for t in range(2))
+        pair_codes, pair_scales = quantize(nc, keep, w1w[1][:].rearrange("p t m j -> p (t m) j"), "w1q_pair")
+        w1q.extend((pair_codes[:, t * P : (t + 1) * P], pair_scales[:, t * P : (t + 1) * P]) for t in range(2))
 
         w2w = woven_tile(N, "w2w")
         weave(nc.vector.tensor_copy, w2w[:], w2r[:])
@@ -115,16 +116,16 @@ def tile_picked_lapl_silu_e_kernel(tc, xT, w1, w2, gate, offs, cen, pos1, pos2, 
         for a in range(2):
             acc = psum.tile([P, HALF], F32, tag="acc", bufs=4, name="acc0_%d" % a)
             mx(nc, acc[:], w1q[0], allc, xq[a])
-            nc.scalar.activation(out=h[0][:, HALF * a : HALF * (a + 1)], in_=acc[:], func=ACT.Silu, bias=0.0 if a else zero[:])
+            nc.scalar.activation(out=h[0][:, HALF * a : HALF * (a + 1)], in_=acc[:], func=ACT.Silu)
         for t in range(1, PACK):
             acc = psum.tile([P, 2, HALF], F32, tag="acc", bufs=4, name="acc%d" % t)
             for a in range(2):
                 mx(nc, acc[:, a, :], w1q[t], allc, xq[a])
-            nc.scalar.activation(out=h[t][:], in_=acc[:].rearrange("p a s -> p (a s)"), func=ACT.Silu)
+            nc.scalar.activation(out=h[t][:], in_=acc[:].rearrange("p a s -> p (a s)"), func=ACT.Silu, bias=zero[:] if t == PACK - 1 else 0.0)
 
         last = PACK - 1
         fetched = keep.tile([P, 2, V], F32, name="fetched")
-        own = keep.tile([P, PACK, V], F32, name="own")
+        own = keep.tile([P, PACK, V], F32, name="own", tag="zero")
         fetched2 = keep.tile([P, V - FUSED_TARGETS], F32, name="fetched2")
         scalar_gather(out=fetched2[:], in_=h[2][:].indirect(pos_t[1][:, FUSED_TARGETS // 16 :]))
         for d in range(2):
@@ -148,13 +149,12 @@ def tile_picked_lapl_silu_e_kernel(tc, xT, w1, w2, gate, offs, cen, pos1, pos2, 
             out=prod[:, 2, 1, 0:FUSED_TARGETS], in0=h[2][:].indirect(pos_t[1][:, 0 : FUSED_TARGETS // 16]),
             in1=gate_t[:, 1, 0:FUSED_TARGETS], op=ALU.mult,
         )
-        add_pair(slice(0, 2), slice(0, V))
         nc.vector.tensor_tensor(out=prod[:, 2, 1, FUSED_TARGETS:V], in0=fetched2[:], in1=gate_t[:, 1, FUSED_TARGETS:V], op=ALU.mult)
         for a in range(2):
             cols = slice(a * P, (a + 1) * P)
             nc.vector.tensor_tensor(out=prod[:, last, :, cols], in0=fetched[:, :, cols], in1=gate_t[:, :, cols], op=ALU.mult)
         for a in range(2):
-            add_pair(slice(2, 4), slice(a * P, (a + 1) * P))
+            add_pair(slice(0, PACK), slice(a * P, (a + 1) * P))
 
         out_v = out.rearrange("(c p) v -> p c v", p=P)
         zw = [woven_tile(P, "zw%d" % a) for a in range(2)]

@@ -18,7 +18,7 @@ P = 128
 PACK = 4
 HALF = S // 2
 W1_VECTOR_SHARE = 88
-FUSED_TARGETS = 64
+FUSED_TARGETS = 96
 
 
 def weave(copy, woven, rows):

@@ -18,7 +18,7 @@ P = 128
 PACK = 4
 HALF = S // 2
 W1_VECTOR_SHARE = 88
-FUSED_TARGETS = 96
+FUSED_TARGETS = 128
 
 
 def weave(copy, woven, rows):
@@ -130,7 +130,7 @@ def tile_picked_lapl_silu_e_kernel(tc, xT, w1, w2, gate, offs, cen, pos1, pos2, 
         scalar_gather(out=fetched2[:], in_=h[2][:].indirect(pos_t[1][:, FUSED_TARGETS // 16 :]))
         for d in range(2):
             scalar_gather(out=fetched[:, d, :], in_=h[last][:].indirect(pos_t[d][:]))
-        for lo, n, tiles in ((0, V, (0,)), (0, P, (1, 2, 3)), (P, P, (1,)), (P, P // 2, (2, 3)), (P + P // 2, P // 2, (2, 3))):
+        for lo, n, tiles in ((0, V, (0,)), (0, P + P // 2, (1,)), (0, P, (2, 3)), (P, P, (2,)), (P, P // 2, (3,)), (P + P // 2, P // 2, (1, 3))):
             for t in tiles:
                 scalar_gather(out=own[:, t, lo : lo + n], in_=h[t][:].indirect(cen_t[:, lo // 16 : (lo + n) // 16]))
 

@@ -18,7 +18,7 @@ P = 128
 PACK = 4
 HALF = S // 2
 W1_VECTOR_SHARE = 88
-FUSED_TARGETS = 128
+FUSED_TARGETS = 96
 
 
 def weave(copy, woven, rows):

@@ -113,15 +113,14 @@ def tile_picked_lapl_silu_e_kernel(tc, xT, w1, w2, gate, offs, cen, pos1, pos2, 
 
         h = [keep.tile([P, S], F32, name="h%d" % t) for t in range(PACK)]
         allc = slice(0, P)
-        for a in range(2):
-            acc = psum.tile([P, HALF], F32, tag="acc", bufs=4, name="acc0_%d" % a)
-            mx(nc, acc[:], w1q[0], allc, xq[a])
-            nc.scalar.activation(out=h[0][:, HALF * a : HALF * (a + 1)], in_=acc[:], func=ACT.Silu)
-        for t in range(1, PACK):
-            acc = psum.tile([P, 2, HALF], F32, tag="acc", bufs=4, name="acc%d" % t)
+        for t in range(PACK):
             for a in range(2):
-                mx(nc, acc[:, a, :], w1q[t], allc, xq[a])
-            nc.scalar.activation(out=h[t][:], in_=acc[:].rearrange("p a s -> p (a s)"), func=ACT.Silu, bias=zero[:] if t == PACK - 1 else 0.0)
+                acc = psum.tile([P, HALF], F32, tag="acc", bufs=4, name="acc%d_%d" % (t, a))
+                mx(nc, acc[:], w1q[t], allc, xq[a])
+                nc.scalar.activation(
+                    out=h[t][:, HALF * a : HALF * (a + 1)], in_=acc[:], func=ACT.Silu,
+                    bias=zero[:] if (t, a) == (PACK - 1, 1) else 0.0,
+                )
 
         last = PACK - 1
         fetched = keep.tile([P, 2, V], F32, name="fetched")

@@ -115,7 +115,7 @@ def tile_picked_lapl_silu_e_kernel(tc, xT, w1, w2, gate, offs, cen, pos1, pos2, 
         allc = slice(0, P)
         for t in range(PACK):
             for a in range(2):
-                acc = psum.tile([P, HALF], F32, tag="acc", bufs=4, name="acc%d_%d" % (t, a))
+                acc = psum.tile([P, HALF], F32, tag="bank", bufs=8, name="acc%d_%d" % (t, a))
                 mx(nc, acc[:], w1q[t], allc, xq[a])
                 nc.scalar.activation(
                     out=h[t][:, HALF * a : HALF * (a + 1)], in_=acc[:], func=ACT.Silu,
@@ -180,13 +180,18 @@ def tile_picked_lapl_silu_e_kernel(tc, xT, w1, w2, gate, offs, cen, pos1, pos2, 
                 out=codes[:, piece].bitcast(FP8X4), scales=scales[:, piece],
                 in_=zw[1][:, piece].rearrange("p w j -> p (w j)"),
             )
-        for a in range(2):
-            o = keep.tile([P, 2, P], F32, name="o%d" % a)
-            for c, copy in enumerate((nc.scalar.copy, nc.vector.tensor_copy if a else nc.scalar.copy)):
-                res = psum.tile([P, P], F32, tag="res", bufs=4, name="res%d_%d" % (a, c))
-                mx(nc, res[:], w2q, slice(c * P, (c + 1) * P), zq[a])
-                copy(out=o[:, c, :], in_=res[:])
-                if a:
-                    nc.sync.dma_start(out_v[:, c, P:V], o[:, c, :])
-            if not a:
-                nc.sync.dma_start(out_v[:, :, 0:P], o[:])
+        o = [keep.tile([P, 2, P], F32, name="o%d" % a) for a in range(2)]
+
+        def project(a, c, cols, copy):
+            res = psum.tile([P, cols.stop - cols.start], F32, tag="bank", bufs=8, name="res%d_%d_%d" % (a, c, cols.start))
+            mx(nc, res[:], w2q, slice(c * P, (c + 1) * P), (zq[a][0][:, cols], zq[a][1][:, cols]))
+            copy(out=o[a][:, c, cols], in_=res[:])
+
+        for c in range(2):
+            project(0, c, allc, nc.scalar.copy)
+        nc.sync.dma_start(out_v[:, :, 0:P], o[0][:])
+        for c in range(2):
+            project(1, c, slice(0, P // 2), nc.scalar.copy)
+        for c, copy in enumerate((nc.scalar.copy, nc.vector.tensor_copy)):
+            project(1, c, slice(P // 2, P), copy)
+            nc.sync.dma_start(out_v[:, c, P:V], o[1][:, c, :])

@@ -17,7 +17,8 @@ ALU = mybir.AluOpType
 P = 128
 PACK = 4
 HALF = S // 2
-W1_VECTOR_SHARE = 88
+W1_VECTOR_SHARE = 76
+W1_VECTOR_FILL = 40
 FUSED_TARGETS = 96
 
 
@@ -102,8 +103,8 @@ def tile_picked_lapl_silu_e_kernel(tc, xT, w1, w2, gate, offs, cen, pos1, pos2, 
         weave_w1(nc.vector.tensor_copy, 0, 0, W1_VECTOR_SHARE)
         weave_w1(nc.scalar.copy, 0, W1_VECTOR_SHARE, P)
         w1q = [quantize(nc, keep, w1w[0][:, t], "w1q%d" % t) for t in range(2)]
-        weave_w1(nc.vector.tensor_copy, 1, 0, P - W1_VECTOR_SHARE)
-        weave_w1(nc.scalar.copy, 1, P - W1_VECTOR_SHARE, P)
+        weave_w1(nc.vector.tensor_copy, 1, 0, W1_VECTOR_FILL)
+        weave_w1(nc.scalar.copy, 1, W1_VECTOR_FILL, P)
         pair_codes, pair_scales = quantize(nc, keep, w1w[1][:].rearrange("p t m j -> p (t m) j"), "w1q_pair")
         w1q.extend((pair_codes[:, t * P : (t + 1) * P], pair_scales[:, t * P : (t + 1) * P]) for t in range(2))
 

from contextlib import ExitStack

import concourse.mybir as mybir

K, T, S, V, H, N = 512, 1024, 512, 256, 512, 256
FLOPS = 2 * K * H * S + 2 * H * N * V

F32 = mybir.dt.float32
BF16 = mybir.dt.bfloat16
U32 = mybir.dt.uint32
U16 = mybir.dt.uint16
U8 = mybir.dt.uint8
FP8X4 = mybir.dt.float8_e4m3fn_x4
ACT = mybir.ActivationFunctionType
ALU = mybir.AluOpType

P = 128
PACK = 4
HALF = S // 2
W1_VECTOR_SHARE = 76
W1_VECTOR_FILL = 40
FUSED_TARGETS = 96


def weave(copy, woven, rows):
    copy(
        out=woven.rearrange("p (c i) j -> p c j i", i=4),
        in_=rows.rearrange("p j (c i) -> p c j i", i=4),
    )


def quantize(nc, pool, woven, name, tag=""):
    width = woven.shape[1]
    codes = pool.tile([P, width], U32, align_bytes=64, name=name + "_codes", tag=tag)
    scales = pool.tile([P, width], U8, align_bytes=64, name=name + "_scales")
    nc.vector.quantize_mx(out=codes[:].bitcast(FP8X4), scales=scales[:], in_=woven.rearrange("p w j -> p (w j)"))
    return codes, scales


def mx(nc, out, lhs, cols, rhs):
    nc.tensor.matmul_mx(
        out=out, lhsT=lhs[0][:, cols].bitcast(FP8X4), lhsT_scale=lhs[1][:, cols],
        rhs=rhs[0][:].bitcast(FP8X4), rhs_scale=rhs[1][:], start=True, stop=True,
    )


def tile_picked_lapl_silu_e_kernel(tc, xT, w1, w2, gate, offs, cen, pos1, pos2, out):
    nc = tc.nc
    with ExitStack() as ctx:
        lists = ctx.enter_context(tc.tile_pool(name="lists", bufs=1))
        keep = ctx.enter_context(tc.tile_pool(name="keep", bufs=1))
        psum = ctx.enter_context(tc.psum_pool(name="psum", bufs=1))

        offs_t = lists.tile([P, S // 16], U16, name="offs_t")
        cen_t = lists.tile([P, V // 16], U16, name="cen_t")
        pos_t = [lists.tile([P, V // 16], U16, name="pos%d_t" % d) for d in range(2)]

        x_rows = xT.rearrange("(p j) t -> p j t", j=PACK)
        xp = [keep.tile([P, T], F32, align_bytes=64, name="xp%d" % j, tag="xp%d" % j) for j in range(PACK)]
        w1r = keep.tile([P, PACK, H], F32, name="w1r")
        w2r = keep.tile([P, PACK, N], F32, name="w2r")
        gate_t = keep.tile([P, 2, V], F32, name="gate_t")

        nc.sync.dma_start(xp[0][:], x_rows[:, 0, :])
        nc.sync.dma_start(offs_t[:], offs)
        for j in range(1, PACK):
            nc.sync.dma_start(xp[j][:], x_rows[:, j, :])
        nc.sync.dma_start(w1r[:], w1.rearrange("(p j) i -> p j i", j=PACK))
        nc.sync.dma_start(w2r[:], w2.rearrange("(p j) m -> p j m", j=PACK))
        nc.sync.dma_start(gate_t[:], gate.rearrange("d p v -> p d v"))
        nc.sync.dma_start(pos_t[0][:], pos1)
        nc.sync.dma_start(pos_t[1][:], pos2)
        nc.sync.dma_start(cen_t[:], cen)

        zero_in = keep.tile([P, 1], F32, name="zero_in")
        zero = keep.tile([P, 1], F32, name="zero", tag="zero")
        nc.gpsimd.memset(zero_in[:], 0.0)
        nc.scalar.activation(out=zero[:], in_=zero_in[:], func=ACT.Silu)

        def woven_tile(width, name):
            return keep.tile([P, width, PACK], BF16, align_bytes=64, name=name)

        def scalar_gather(out, in_):
            nc.scalar.activation(out=out, in_=in_, func=ACT.Copy)

        xw = [woven_tile(HALF, "xw%d" % a) for a in range(2)]
        xg = keep.tile([P, PACK, HALF], BF16, name="xg")
        for j in range(PACK):
            nc.vector.tensor_copy(out=xw[0][:, :, j], in_=xp[j][:].indirect(offs_t[:, 0 : HALF // 16]))
            for lo, n in ((0, HALF),) if j < PACK - 1 else ((0, P), (P, P)):
                first = (HALF + lo) // 16
                scalar_gather(out=xg[:, j, lo : lo + n], in_=xp[j][:].indirect(offs_t[:, first : first + n // 16]))
        weave(nc.scalar.copy, xw[1][:, 0:P], xg[:, :, 0:P])
        weave(nc.vector.tensor_copy, xw[1][:, P:HALF], xg[:, :, P:HALF])
        xq = [quantize(nc, keep, xw[0][:], "xq0", "xp3"), quantize(nc, keep, xw[1][:], "xq1")]

        w1_cols = w1r[:].rearrange("p j (m t) -> p m j t", t=PACK)
        w1w = [keep.tile([P, 2, P, PACK], BF16, align_bytes=64, name="w1w%d" % u) for u in range(2)]

        def weave_w1(copy, u, lo, hi):
            copy(out=w1w[u][:].rearrange("p t m j -> p m j t")[:, lo:hi], in_=w1_cols[:, lo:hi, :, 2 * u : 2 * u + 2])

        weave_w1(nc.vector.tensor_copy, 0, 0, W1_VECTOR_SHARE)
        weave_w1(nc.scalar.copy, 0, W1_VECTOR_SHARE, P)
        w1q = [quantize(nc, keep, w1w[0][:, t], "w1q%d" % t) for t in range(2)]
        weave_w1(nc.vector.tensor_copy, 1, 0, W1_VECTOR_FILL)
        weave_w1(nc.scalar.copy, 1, W1_VECTOR_FILL, P)
        pair_codes, pair_scales = quantize(nc, keep, w1w[1][:].rearrange("p t m j -> p (t m) j"), "w1q_pair")
        w1q.extend((pair_codes[:, t * P : (t + 1) * P], pair_scales[:, t * P : (t + 1) * P]) for t in range(2))

        w2w = woven_tile(N, "w2w")
        weave(nc.vector.tensor_copy, w2w[:], w2r[:])
        w2q = quantize(nc, keep, w2w[:], "w2q")

        h = [keep.tile([P, S], F32, name="h%d" % t) for t in range(PACK)]
        allc = slice(0, P)
        for t in range(PACK):
            for a in range(2):
                acc = psum.tile([P, HALF], F32, tag="bank", bufs=8, name="acc%d_%d" % (t, a))
                mx(nc, acc[:], w1q[t], allc, xq[a])
                nc.scalar.activation(
                    out=h[t][:, HALF * a : HALF * (a + 1)], in_=acc[:], func=ACT.Silu,
                    bias=zero[:] if (t, a) == (PACK - 1, 1) else 0.0,
                )

        last = PACK - 1
        fetched = keep.tile([P, 2, V], F32, name="fetched")
        own = keep.tile([P, PACK, V], F32, name="own", tag="zero")
        fetched2 = keep.tile([P, V - FUSED_TARGETS], F32, name="fetched2")
        scalar_gather(out=fetched2[:], in_=h[2][:].indirect(pos_t[1][:, FUSED_TARGETS // 16 :]))
        for d in range(2):
            scalar_gather(out=fetched[:, d, :], in_=h[last][:].indirect(pos_t[d][:]))
        for lo, n, tiles in ((0, V, (0,)), (0, P + P // 2, (1,)), (0, P, (2, 3)), (P, P, (2,)), (P, P // 2, (3,)), (P + P // 2, P // 2, (1, 3))):
            for t in tiles:
                scalar_gather(out=own[:, t, lo : lo + n], in_=h[t][:].indirect(cen_t[:, lo // 16 : (lo + n) // 16]))

        prod = keep.tile([P, PACK, 2, V], F32, name="prod")
        pull = keep.tile([P, PACK, V], F32, name="pull")

        def weighted(t, d):
            nc.vector.tensor_tensor(out=prod[:, t, d, :], in0=h[t][:].indirect(pos_t[d][:]), in1=gate_t[:, d, :], op=ALU.mult)

        def add_pair(tiles, cols):
            nc.vector.tensor_tensor(out=pull[:, tiles, cols], in0=prod[:, tiles, 0, cols], in1=prod[:, tiles, 1, cols], op=ALU.add)

        for t, d in ((0, 0), (0, 1), (1, 0), (1, 1), (2, 0)):
            weighted(t, d)
        nc.vector.tensor_tensor(
            out=prod[:, 2, 1, 0:FUSED_TARGETS], in0=h[2][:].indirect(pos_t[1][:, 0 : FUSED_TARGETS // 16]),
            in1=gate_t[:, 1, 0:FUSED_TARGETS], op=ALU.mult,
        )
        nc.vector.tensor_tensor(out=prod[:, 2, 1, FUSED_TARGETS:V], in0=fetched2[:], in1=gate_t[:, 1, FUSED_TARGETS:V], op=ALU.mult)
        for a in range(2):
            cols = slice(a * P, (a + 1) * P)
            nc.vector.tensor_tensor(out=prod[:, last, :, cols], in0=fetched[:, :, cols], in1=gate_t[:, :, cols], op=ALU.mult)
        for a in range(2):
            add_pair(slice(0, PACK), slice(a * P, (a + 1) * P))

        out_v = out.rearrange("(c p) v -> p c v", p=P)
        zw = [woven_tile(P, "zw%d" % a) for a in range(2)]

        def subtract(a, lo, n):
            cols = slice(a * P + lo, a * P + lo + n)
            nc.vector.tensor_tensor(
                out=zw[a][:, lo : lo + n].rearrange("p (c i) j -> p c j i", i=4),
                in0=own[:, :, cols].rearrange("p j (c i) -> p c j i", i=4),
                in1=pull[:, :, cols].rearrange("p j (c i) -> p c j i", i=4),
                op=ALU.subtract,
            )

        subtract(0, 0, P)
        subtract(1, 0, P // 2)
        zq = [quantize(nc, keep, zw[0][:], "zq0")]
        subtract(1, P // 2, P // 2)
        codes = keep.tile([P, P], U32, align_bytes=64, name="zq1_codes")
        scales = keep.tile([P, P], U8, align_bytes=64, name="zq1_scales")
        zq.append((codes, scales))
        for lo in (0, P // 2):
            piece = slice(lo, lo + P // 2)
            nc.vector.quantize_mx(
                out=codes[:, piece].bitcast(FP8X4), scales=scales[:, piece],
                in_=zw[1][:, piece].rearrange("p w j -> p (w j)"),
            )
        o = [keep.tile([P, 2, P], F32, name="o%d" % a) for a in range(2)]

        def project(a, c, cols, copy):
            res = psum.tile([P, cols.stop - cols.start], F32, tag="bank", bufs=8, name="res%d_%d_%d" % (a, c, cols.start))
            mx(nc, res[:], w2q, slice(c * P, (c + 1) * P), (zq[a][0][:, cols], zq[a][1][:, cols]))
            copy(out=o[a][:, c, cols], in_=res[:])

        for c in range(2):
            project(0, c, allc, nc.scalar.copy)
        nc.sync.dma_start(out_v[:, :, 0:P], o[0][:])
        for c in range(2):
            project(1, c, slice(0, P // 2), nc.scalar.copy)
        for c, copy in enumerate((nc.scalar.copy, nc.vector.tensor_copy)):
            project(1, c, slice(P // 2, P), copy)
            nc.sync.dma_start(out_v[:, c, P:V], o[1][:, c, :])
